import numpy as np, ml_dtypes
CORES = [33,161,289,417,57,185,313,441]
N = 8
import mx_ref
NC = 256
A = np.float32(0.03)
BF = ml_dtypes.bfloat16
def setup_inputs(rng):
    def f(*shape):
        return mx_ref.flush((rng.standard_normal(shape, dtype=np.float32) * np.exp2(rng.integers(-2, 3, shape[:-1] + (1,)))).astype(BF))
    tg = np.stack([rng.integers(0, N, (N, 128)), rng.integers(0, NC, (N, 128))], axis=2).astype(BF)
    return {"tg": tg, "x": f(N, 128, 512), "w": f(N, 128, 4 * NC)}
def setup_inputs_blocks(rng):
    d = setup_inputs(rng)
    for k in ("x", "w"): d[k] = mx_ref.spread(d[k], rng, 2)
    return d
def setup_inputs_sharp(rng):
    d = setup_inputs(rng); d["w"] = (d["w"].astype(np.float32) * 32).astype(BF)
    return d
def setup_inputs_apart(rng):
    d = setup_inputs(rng); d["w"] = mx_ref.flush((d["w"].astype(np.float32) * np.exp2(rng.permutation(np.linspace(-3, 3, N))).astype(np.float32).reshape(N, 1, 1)).astype(BF))
    return d
def reference(tg, x, w):
    W = [mx_ref.quantize(w[r]) for r in range(N)]
    y = np.zeros((N, 128, 2), np.float32)
    for j in range(N):
        X = mx_ref.quantize(x[j])
        L = [(mx_ref.matmul(X, W[r]) * A).astype(np.float64) for r in range(N)]
        m = np.max([l.max(axis=1, keepdims=True) for l in L], axis=0); s = sum(np.exp(l - m).sum(axis=1, keepdims=True) for l in L)
        t = np.array([[L[int(a) % N][i, int(c) % NC]] for i, (a, c) in enumerate(tg[j].astype(np.float32))])
        y[j] = np.concatenate([np.log(s) + m - t, np.log(s) + m], axis=1).astype(np.float32)
    return {"y": y}

@@ -1,0 +1,264 @@
+import math
+import numpy as np
+from concourse.bass import DstId, RemoteDMATransfer
+from concourse.mybir import dt, AluOpType, AxisListType, ActivationFunctionType
+
+NC = 256
+NX = 128
+SCALE = float(np.float32(0.03))
+K, DEG, STEP = 16, 7, 0.5
+B = DEG + 1
+
+SCRATCH = {
+    "win": ("sbuf", [128, 4 * NC], "bfloat16"),
+    "xin": ("sbuf", [128, 4 * NX], "bfloat16"),
+    "tgo": ("sbuf", [128, 8], "bfloat16"),
+    "tgp": ("sbuf", [128, 8], "bfloat16"),
+    "wc": ("sbuf", [128, 4 * NC], "float8_e4m3fn_x4"),
+    "ws": ("sbuf", [128, 4 * NC], "uint8"),
+    "xc": ("sbuf", [128, 2 * NX], "float8_e4m3fn_x4"),
+    "xs": ("sbuf", [128, 2 * NX], "uint8"),
+    "ps": ("psum", [128, 4096], "float32"),
+    "col": ("sbuf", [128, NC], "bfloat16"),
+    "mk": ("sbuf", [128, 8 * NC], "bfloat16"),
+    "ex": ("sbuf", [128, 4 * NC], "float32"),
+    "pr": ("sbuf", [128, 4 * NC], "float32"),
+    "vo": ("sbuf", [128, 4], "float32"),
+    "vp": ("sbuf", [128, 4], "float32"),
+    "mxb": ("sbuf", [128, 8], "float32"),
+    "st": ("sbuf", [128, 24], "float32"),
+    "sp": ("sbuf", [128, 12], "float32"),
+    "e0": ("sbuf", [128, K * B], "float32"),
+    "d1": ("sbuf", [128, K * B], "float32"),
+    "d0": ("sbuf", [128, K * B], "float32"),
+    "sc": ("sbuf", [128, K * B], "float32"),
+    "f": ("sbuf", [128, 32], "float32"),
+    "yt": ("sbuf", [128, 4], "float32"),
+}
+TILES = [("o", 0), ("p", 0), ("p", 1), ("o", 1), ("p", 2), ("p", 3), ("o", 2), ("o", 3)]
+SEMAPHORES = (["lw", "lx", "lt", "qw", "qx", "io", "kc", "vo", "vp", "mko", "mkp", "loc", "rin",
+               "c1", "s1", "c2", "s2", "c3", "s3", "pxc", "pxs", "ptg", "pst",
+               "f1", "f2", "f3", "f4", "f5", "f6", "f7", "f8", "f9", "fm", "stored"]
+              + [n + str(i) for i in range(8) for n in ("mm", "mx", "nb", "ex", "pr", "cp")])
+
+
+def roles(c, T, topo):
+    rk = topo.rack(topo.host(c))
+    near = [q for q in T.cores if q != c and topo.rack(topo.host(q)) == rk]
+    sib = [q for q in near if topo.same_plane(c, q)][0]
+    partner = [q for q in T.cores if topo.rack(topo.host(q)) != rk and topo.chip(q) == topo.chip(c) and topo.may_write(c, q)][0]
+    cross = [q for q in near if not topo.same_plane(c, q)]
+    same = [q for q in cross if topo.host(q) == topo.host(c)][0]
+    other = [q for q in cross if topo.host(q) != topo.host(c)][0]
+    base = [h for h in range(512) if topo.host(h) == topo.host(c) and topo.chip(h) == topo.chip(c) and T.rank_of(h) is None
+            and topo.may_write(h, same) and topo.may_write(h, other)]
+    mine = [h for h in base if topo.die(h) == topo.die(c)]
+    far = [h for h in base if topo.die(h) != topo.die(c)]
+    return {"sib": sib, "partner": partner, "same": same, "other": other,
+            "relay": [(mine[0], same, 2, "c"), (far[0], other, 3, "c"), (mine[1], same, 2, "s"), (far[1], other, 3, "s")]}
+
+
+def split(mask, n):
+    bits = [b for b in range(16) if mask >> b & 1]
+    k = len(bits) // n
+    return [sum(1 << b for b in bits[i * k:(i + 1) * k]) for i in range(n)]
+
+
+def cnt(mask):
+    return bin(mask).count("1")
+
+
+def piece(T, kind, slot):
+    if kind == "c":
+        return T.wc[:, slot * NC:(slot + 1) * NC].bitcast(dt.uint8)
+    return T.ws[:, slot * NC:(slot + 1) * NC]
+
+
+def relay_program(g, core, T, topo):
+    for c in T.cores:
+        if (topo.host(c), topo.chip(c)) != (topo.host(core), topo.chip(core)):
+            continue
+        for h, dst, slot, kind in roles(c, T, topo)["relay"]:
+            if h == core:
+                m_in = split(topo.mask(c, core), 2)[0]
+                m = topo.mask(core, dst)
+                rid, pid = topo.addr(dst, core)
+                g.wait_ge(T.sem["rin"], cnt(m_in))
+                g.remote_dma(piece(T, kind, slot), piece(T, kind, 0), T.sem[kind + str(slot)], T.sem["loc"], pid, rid, m)
+                g.wait_ge(T.sem["loc"], cnt(m))
+
+
+def rank_program(g, core, T, topo):
+    rank = T.rank_of(core)
+    if rank is None:
+        relay_program(g, core, T, topo)
+        return
+    R = roles(core, T, topo)
+    S = T.sem
+    A = AluOpType
+    F = ActivationFunctionType
+    X = AxisListType.X
+    partner, sib = R["partner"], R["sib"]
+    slot_rank = [T.rank_of(q) for q in (core, sib, R["same"], R["other"])]
+    m_par, m_sib = topo.mask(core, partner), topo.mask(core, sib)
+    n_par, n_sib = cnt(m_par), cnt(m_sib)
+
+    g.sync.dma_start(T.win[:], T.w[:]).then_inc(S["lw"], 16)
+    g.scalar.dma_start(T.xin[:], T.x[:]).then_inc(S["lx"], 16)
+    g.sync.dma_start(T.tgo[:, 0:2], T.tg[:]).then_inc(S["lt"], 16)
+
+    g.iota(T.col[:], [[1, NC]], 0, 0, allow_small_or_imprecise_dtypes=True).then_inc(S["io"], 1)
+    local = [0]
+
+    def fused(kind, pair):
+        ms = split(topo.mask(core, pair[0][0]), 2)
+        tr = []
+        for (h, dst, slot, k), m in zip(pair, ms):
+            rid, pid = topo.addr(h, core)
+            tr.append(RemoteDMATransfer(dst_ids=[DstId(rid=rid, pnc=pid)], dma_engine_mask=m, remote_sem=S["rin"],
+                                        src=piece(T, kind, 0), dst=piece(T, kind, 0)))
+            local[0] += cnt(m)
+        g.remote_dma_fused(tr, local_sem=S["loc"])
+
+    def send(out, in_, sem, dst):
+        m = topo.mask(core, dst)
+        rid, pid = topo.addr(dst, core)
+        g.remote_dma(out, in_, S[sem], S["loc"], pid, rid, m)
+        local[0] += cnt(m)
+
+    g.wait_ge(S["qw"], 1)
+    fused("c", R["relay"][0:2])
+    fused("s", R["relay"][2:4])
+    g.wait_ge(S["qx"], 1)
+    send(T.xc[:, NX:2 * NX].bitcast(dt.uint8), T.xc[:, 0:NX].bitcast(dt.uint8), "pxc", partner)
+    send(T.xs[:, NX:2 * NX], T.xs[:, 0:NX], "pxs", partner)
+    g.wait_ge(S["lt"], 16)
+    send(T.tgp[:, 0:2], T.tgo[:, 0:2], "ptg", partner)
+    send(piece(T, "c", 1), piece(T, "c", 0), "c1", sib)
+    send(piece(T, "s", 1), piece(T, "s", 0), "s1", sib)
+    for i, (who, slot) in enumerate(TILES):
+        if who == "p":
+            g.wait_ge(S["ex%d" % i], 1)
+            g.wait_ge(S["cp%d" % i], 1)
+    send(T.st[:, 12:24], T.sp[:], "pst", partner)
+    g.wait_ge(S["loc"], local[0])
+
+    g.tensor.wait_ge(S["qw"], 1)
+    g.tensor.wait_ge(S["qx"], 1)
+    n_in = {2: cnt(topo.mask(R["relay"][0][0], R["same"])), 3: cnt(topo.mask(R["relay"][1][0], R["other"])), 1: n_sib}
+    seen = set()
+    for i, (who, slot) in enumerate(TILES):
+        if who == "p" and "p" not in seen:
+            g.tensor.wait_ge(S["pxc"], n_par)
+            g.tensor.wait_ge(S["pxs"], n_par)
+            seen.add("p")
+        if slot and slot not in seen:
+            g.tensor.wait_ge(S["c%d" % slot], n_in[slot])
+            g.tensor.wait_ge(S["s%d" % slot], n_in[slot])
+            seen.add(slot)
+        a, b = (0, NX) if who == "o" else (NX, 2 * NX)
+        c, d = slot * NC, (slot + 1) * NC
+        g.tensor.matmul_mx(T.ps[:, 512 * i:512 * i + NC], T.xc[:, a:b], T.xs[:, a:b], T.wc[:, c:d], T.ws[:, c:d],
+                           True, True).then_inc(S["mm%d" % i], 1)
+
+    def stat(who, slot, k):
+        buf = T.st if who == "o" else T.sp
+        return buf[:, 3 * slot + k:3 * slot + k + 1]
+
+    def bank(i):
+        return T.ps[:, 512 * i:512 * i + NC]
+
+    def reg(buf, i):
+        return buf[:, (i % 4) * NC:(i % 4 + 1) * NC]
+
+    def mask(who, slot):
+        o = slot * NC + (0 if who == "o" else 4 * NC)
+        return T.mk[:, o:o + NC]
+
+    v = g.vector
+    v.wait_ge(S["lw"], 16)
+    v.quantize_mx(T.wc[:, 0:NC], T.ws[:, 0:NC], T.win[:]).then_inc(S["qw"], 1)
+    v.wait_ge(S["lx"], 16)
+    v.quantize_mx(T.xc[:, 0:NX], T.xs[:, 0:NX], T.xin[:]).then_inc(S["qx"], 1)
+
+    def masks(who, tgbuf, vbuf, vsem, msem):
+        v.tensor_scalar(vbuf[:, 0:1], tgbuf[:, 0:1], float(NC), tgbuf[:, 1:2], A.mult, A.add).then_inc(S[vsem], 1)
+        v.wait_ge(S[vsem], 1)
+        for slot in range(4):
+            v.tensor_scalar(mask(who, slot), T.col[:], float(NC * slot_rank[slot]), vbuf[:, 0:1], A.add, A.is_equal).then_inc(S[msem], 1)
+
+    coef = [0.0] * B
+    for n in range(1, B):
+        for j in range(n + 1):
+            coef[j] += (-1.0) ** (n + 1) / n * math.comb(n, j) * (-1.0) ** (n - j)
+    nk = 0
+    v.memset(T.e0[:, 0:K * B:B], 0.0).then_inc(S["kc"], 1)
+    for j in range(DEG):
+        v.memset(T.d1[:, j:K * B:B], coef[DEG - j]).then_inc(S["kc"], 1)
+    for k in range(K):
+        v.memset(T.e0[:, k * B + 1:(k + 1) * B], math.exp(-STEP * k)).then_inc(S["kc"], 1)
+        v.memset(T.d1[:, k * B + DEG:(k + 1) * B], coef[0] + STEP * k).then_inc(S["kc"], 1)
+    nk = 1 + DEG + 2 * K
+    v.wait_ge(S["io"], 1)
+    v.wait_ge(S["lt"], 16)
+    masks("o", T.tgo, T.vo, "vo", "mko")
+    v.wait_ge(S["ptg"], n_par)
+    masks("p", T.tgp, T.vp, "vp", "mkp")
+    v.wait_ge(S["mko"], 4)
+    v.wait_ge(S["mkp"], 4)
+    for first in range(0, 8, 2):
+        for i in (first, first + 1):
+            who, slot = TILES[i]
+            v.wait_ge(S["mm%d" % i], 1)
+            v.tensor_reduce(T.mxb[:, i:i + 1], bank(i), X, A.max).then_inc(S["mx%d" % i], 1)
+            v.wait_ge(S["mx%d" % i], 1)
+            v.tensor_scalar(stat(who, slot, 0), T.mxb[:, i:i + 1], -SCALE, None, A.mult).then_inc(S["nb%d" % i], 1)
+        for i in (first, first + 1):
+            who, slot = TILES[i]
+            v.wait_ge(S["ex%d" % i], 1)
+            if i >= 4:
+                v.wait_ge(S["cp%d" % (i - 4)], 1)
+            v.tensor_tensor(reg(T.pr, i), bank(i), mask(who, slot), A.mult).then_inc(S["pr%d" % i], 1)
+
+    s = g.scalar
+    for first in range(0, 8, 2):
+        for i in (first, first + 1):
+            who, slot = TILES[i]
+            s.wait_ge(S["nb%d" % i], 1)
+            s.activation(reg(T.ex, i), bank(i), F.Exp, bias=stat(who, slot, 0), scale=SCALE,
+                         accum_out=stat(who, slot, 1)).then_inc(S["ex%d" % i], 1)
+        for i in (first, first + 1):
+            who, slot = TILES[i]
+            s.wait_ge(S["pr%d" % i], 1)
+            s.activation(reg(T.pr, i), reg(T.pr, i), F.Copy, scale=SCALE, accum_out=stat(who, slot, 2)).then_inc(S["cp%d" % i], 1)
+
+    for i, (who, slot) in enumerate(TILES):
+        if who == "o":
+            v.wait_ge(S["cp%d" % i], 1)
+    v.wait_ge(S["kc"], nk)
+    v.wait_ge(S["pst"], n_par)
+    fb = T.f
+    v.tensor_reduce(fb[:, 0:1], T.st[:, 0:24:3], X, A.min).then_inc(S["f1"], 1)
+    v.tensor_reduce(fb[:, 1:2], T.st[:, 2:24:3], X, A.add).then_inc(S["f3"], 1)
+    s.wait_ge(S["f1"], 1)
+    s.activation(fb[:, 8:16], T.st[:, 0:24:3], F.Exp, bias=fb[:, 0:1], scale=-1.0).then_inc(S["f2"], 1)
+    v.wait_ge(S["f1"], 1)
+    v.tensor_scalar(fb[:, 5:6], fb[:, 0:1], -1.0, None, A.mult).then_inc(S["fm"], 1)
+    v.wait_ge(S["f3"], 1)
+    v.tensor_scalar(fb[:, 4:5], fb[:, 0:1], -1.0, fb[:, 1:2], A.mult, A.subtract).then_inc(S["fm"], 1)
+    v.wait_ge(S["f2"], 1)
+    v.tensor_tensor(fb[:, 16:24], fb[:, 8:16], T.st[:, 1:24:3], A.mult).then_inc(S["f4"], 1)
+    v.wait_ge(S["f4"], 1)
+    v.tensor_reduce(fb[:, 2:3], fb[:, 16:24], X, A.add).then_inc(S["f5"], 1)
+    v.wait_ge(S["f5"], 1)
+    v.tensor_scalar(T.d0[:], T.e0[:], fb[:, 2:3], None, A.mult).then_inc(S["f6"], 1)
+    v.wait_ge(S["f6"], 1)
+    v.tensor_tensor_scan(T.sc[:], T.d0[:], T.d1[:], 0.0, A.mult, A.add).then_inc(S["f7"], 1)
+    v.wait_ge(S["f7"], 1)
+    v.tensor_reduce(fb[:, 3:4], T.sc[:, DEG:K * B:B], X, A.min).then_inc(S["f8"], 1)
+    v.wait_ge(S["f8"], 1)
+    v.wait_ge(S["fm"], 2)
+    v.tensor_scalar(T.yt[:, 0:2], fb[:, 4:6], fb[:, 3:4], None, A.add).then_inc(S["f9"], 1)
+    g.sync.wait_ge(S["f9"], 1)
+    g.sync.dma_start(T.y[:], T.yt[:, 0:2]).then_inc(S["stored"], 16)
+    g.sync.wait_ge(S["stored"], 16)

@@ -36,8 +36,8 @@ SCRATCH = {
     "yt": ("sbuf", [128, 4], "float32"),
 }
 TILES = [("o", 0), ("p", 0), ("p", 1), ("o", 1), ("p", 2), ("p", 3), ("o", 2), ("o", 3)]
-SEMAPHORES = (["lw", "lx", "lt", "qw", "qx", "io", "kc", "vo", "vp", "mko", "mkp", "loc", "rin",
-               "c1", "s1", "c2", "s2", "c3", "s3", "pxc", "pxs", "ptg", "pst",
+SEMAPHORES = (["lw", "lx", "lt", "qw", "qx", "io", "kc", "vo", "vp", "mko", "mkp", "loc", "rin", "rx",
+               "c1", "s1", "c2", "s2", "c3", "s3", "pxc", "pxs", "ptg", "pst", "ptt",
                "f1", "f2", "f3", "f4", "f5", "f6", "f7", "f8", "f9", "fm", "stored"]
               + [n + str(i) for i in range(8) for n in ("mm", "mx", "nb", "ex", "pr", "cp")])
 
@@ -68,6 +68,10 @@ def cnt(mask):
     return bin(mask).count("1")
 
 
+def hand(c, R, topo):
+    return split(topo.mask(c, R["relay"][0][0]), 2)
+
+
 def piece(T, kind, slot):
     if kind == "c":
         return T.wc[:, slot * NC:(slot + 1) * NC].bitcast(dt.uint8)
@@ -78,14 +82,24 @@ def relay_program(g, core, T, topo):
     for c in T.cores:
         if (topo.host(c), topo.chip(c)) != (topo.host(core), topo.chip(core)):
             continue
-        for h, dst, slot, kind in roles(c, T, topo)["relay"]:
+        R = roles(c, T, topo)
+        for i, (h, dst, slot, kind) in enumerate(R["relay"]):
             if h == core:
-                m_in = split(topo.mask(c, core), 2)[0]
+                n = 0
+                if i < 2:
+                    p = R["partner"]
+                    m = topo.mask(core, p)
+                    rid, pid = topo.addr(p, core)
+                    g.wait_ge(T.sem["rx"], cnt(hand(c, R, topo)[i]))
+                    o = i * NX // 2
+                    g.remote_dma(T.xc[:, NX + o:NX + o + NX // 2].bitcast(dt.uint8), T.xc[:, o:o + NX // 2].bitcast(dt.uint8),
+                                 T.sem["pxc"], T.sem["loc"], pid, rid, m)
+                    n += cnt(m)
                 m = topo.mask(core, dst)
                 rid, pid = topo.addr(dst, core)
-                g.wait_ge(T.sem["rin"], cnt(m_in))
+                g.wait_ge(T.sem["rin"], cnt(hand(c, R, topo)[i % 2]))
                 g.remote_dma(piece(T, kind, slot), piece(T, kind, 0), T.sem[kind + str(slot)], T.sem["loc"], pid, rid, m)
-                g.wait_ge(T.sem["loc"], cnt(m))
+                g.wait_ge(T.sem["loc"], cnt(m) + n)
 
 
 def rank_program(g, core, T, topo):
@@ -100,23 +114,21 @@ def rank_program(g, core, T, topo):
     X = AxisListType.X
     partner, sib = R["partner"], R["sib"]
     slot_rank = [T.rank_of(q) for q in (core, sib, R["same"], R["other"])]
-    m_par, m_sib = topo.mask(core, partner), topo.mask(core, sib)
-    n_par, n_sib = cnt(m_par), cnt(m_sib)
+    rl = [r[0] for r in R["relay"]]
+    n_par, n_sib = cnt(topo.mask(core, partner)), cnt(topo.mask(core, sib))
 
-    g.sync.dma_start(T.win[:], T.w[:]).then_inc(S["lw"], 16)
     g.scalar.dma_start(T.xin[:], T.x[:]).then_inc(S["lx"], 16)
+    g.sync.dma_start(T.win[:], T.w[:]).then_inc(S["lw"], 16)
     g.sync.dma_start(T.tgo[:, 0:2], T.tg[:]).then_inc(S["lt"], 16)
 
     g.iota(T.col[:], [[1, NC]], 0, 0, allow_small_or_imprecise_dtypes=True).then_inc(S["io"], 1)
     local = [0]
 
-    def fused(kind, pair):
-        ms = split(topo.mask(core, pair[0][0]), 2)
+    def fused(sem, parts):
         tr = []
-        for (h, dst, slot, k), m in zip(pair, ms):
+        for (h, out, in_), m in zip(parts, hand(core, R, topo)):
             rid, pid = topo.addr(h, core)
-            tr.append(RemoteDMATransfer(dst_ids=[DstId(rid=rid, pnc=pid)], dma_engine_mask=m, remote_sem=S["rin"],
-                                        src=piece(T, kind, 0), dst=piece(T, kind, 0)))
+            tr.append(RemoteDMATransfer(dst_ids=[DstId(rid=rid, pnc=pid)], dma_engine_mask=m, remote_sem=S[sem], src=in_, dst=out))
             local[0] += cnt(m)
         g.remote_dma_fused(tr, local_sem=S["loc"])
 
@@ -126,30 +138,33 @@ def rank_program(g, core, T, topo):
         g.remote_dma(out, in_, S[sem], S["loc"], pid, rid, m)
         local[0] += cnt(m)
 
-    g.wait_ge(S["qw"], 1)
-    fused("c", R["relay"][0:2])
-    fused("s", R["relay"][2:4])
     g.wait_ge(S["qx"], 1)
-    send(T.xc[:, NX:2 * NX].bitcast(dt.uint8), T.xc[:, 0:NX].bitcast(dt.uint8), "pxc", partner)
+    fused("rx", [(rl[i], T.xc[:, i * NX // 2:(i + 1) * NX // 2].bitcast(dt.uint8),
+                  T.xc[:, i * NX // 2:(i + 1) * NX // 2].bitcast(dt.uint8)) for i in range(2)])
+    g.wait_ge(S["qw"], 1)
+    fused("rin", [(h, piece(T, "c", 0), piece(T, "c", 0)) for h in rl[0:2]])
+    fused("rin", [(h, piece(T, "s", 0), piece(T, "s", 0)) for h in rl[2:4]])
     send(T.xs[:, NX:2 * NX], T.xs[:, 0:NX], "pxs", partner)
     g.wait_ge(S["lt"], 16)
     send(T.tgp[:, 0:2], T.tgo[:, 0:2], "ptg", partner)
     send(piece(T, "c", 1), piece(T, "c", 0), "c1", sib)
     send(piece(T, "s", 1), piece(T, "s", 0), "s1", sib)
-    for i, (who, slot) in enumerate(TILES):
-        if who == "p":
-            g.wait_ge(S["ex%d" % i], 1)
-            g.wait_ge(S["cp%d" % i], 1)
-    send(T.st[:, 12:24], T.sp[:], "pst", partner)
+    late = [i for i in range(8) if TILES[i][0] == "p"]
+    for i in late:
+        g.wait_ge(S["ex%d" % i], 1)
+    send(T.st[:, 8:16], T.sp[:, 0:8], "pst", partner)
+    for i in late:
+        g.wait_ge(S["cp%d" % i], 1)
+    send(T.st[:, 20:24], T.sp[:, 8:12], "ptt", partner)
     g.wait_ge(S["loc"], local[0])
 
     g.tensor.wait_ge(S["qw"], 1)
     g.tensor.wait_ge(S["qx"], 1)
-    n_in = {2: cnt(topo.mask(R["relay"][0][0], R["same"])), 3: cnt(topo.mask(R["relay"][1][0], R["other"])), 1: n_sib}
+    n_in = {2: cnt(topo.mask(rl[0], R["same"])), 3: cnt(topo.mask(rl[1], R["other"])), 1: n_sib}
     seen = set()
     for i, (who, slot) in enumerate(TILES):
         if who == "p" and "p" not in seen:
-            g.tensor.wait_ge(S["pxc"], n_par)
+            g.tensor.wait_ge(S["pxc"], sum(cnt(topo.mask(h, partner)) for h in rl[0:2]))
             g.tensor.wait_ge(S["pxs"], n_par)
             seen.add("p")
         if slot and slot not in seen:
@@ -162,8 +177,9 @@ def rank_program(g, core, T, topo):
                            True, True).then_inc(S["mm%d" % i], 1)
 
     def stat(who, slot, k):
-        buf = T.st if who == "o" else T.sp
-        return buf[:, 3 * slot + k:3 * slot + k + 1]
+        if k == 2:
+            return T.st[:, 16 + slot:17 + slot] if who == "o" else T.sp[:, 8 + slot:9 + slot]
+        return (T.st if who == "o" else T.sp)[:, 2 * slot + k:2 * slot + k + 1]
 
     def bank(i):
         return T.ps[:, 512 * i:512 * i + NC]
@@ -176,10 +192,10 @@ def rank_program(g, core, T, topo):
         return T.mk[:, o:o + NC]
 
     v = g.vector
-    v.wait_ge(S["lw"], 16)
-    v.quantize_mx(T.wc[:, 0:NC], T.ws[:, 0:NC], T.win[:]).then_inc(S["qw"], 1)
     v.wait_ge(S["lx"], 16)
     v.quantize_mx(T.xc[:, 0:NX], T.xs[:, 0:NX], T.xin[:]).then_inc(S["qx"], 1)
+    v.wait_ge(S["lw"], 16)
+    v.quantize_mx(T.wc[:, 0:NC], T.ws[:, 0:NC], T.win[:]).then_inc(S["qw"], 1)
 
     def masks(who, tgbuf, vbuf, vsem, msem):
         v.tensor_scalar(vbuf[:, 0:1], tgbuf[:, 0:1], float(NC), tgbuf[:, 1:2], A.mult, A.add).then_inc(S[vsem], 1)
@@ -191,7 +207,6 @@ def rank_program(g, core, T, topo):
     for n in range(1, B):
         for j in range(n + 1):
             coef[j] += (-1.0) ** (n + 1) / n * math.comb(n, j) * (-1.0) ** (n - j)
-    nk = 0
     v.memset(T.e0[:, 0:K * B:B], 0.0).then_inc(S["kc"], 1)
     for j in range(DEG):
         v.memset(T.d1[:, j:K * B:B], coef[DEG - j]).then_inc(S["kc"], 1)
@@ -238,22 +253,23 @@ def rank_program(g, core, T, topo):
     v.wait_ge(S["kc"], nk)
     v.wait_ge(S["pst"], n_par)
     fb = T.f
-    v.tensor_reduce(fb[:, 0:1], T.st[:, 0:24:3], X, A.min).then_inc(S["f1"], 1)
-    v.tensor_reduce(fb[:, 1:2], T.st[:, 2:24:3], X, A.add).then_inc(S["f3"], 1)
+    nbs, ss = T.st[:, 0:16:2], T.st[:, 1:16:2]
+    v.tensor_reduce(fb[:, 0:1], nbs, X, A.min).then_inc(S["f1"], 1)
     s.wait_ge(S["f1"], 1)
-    s.activation(fb[:, 8:16], T.st[:, 0:24:3], F.Exp, bias=fb[:, 0:1], scale=-1.0).then_inc(S["f2"], 1)
-    v.wait_ge(S["f1"], 1)
-    v.tensor_scalar(fb[:, 5:6], fb[:, 0:1], -1.0, None, A.mult).then_inc(S["fm"], 1)
-    v.wait_ge(S["f3"], 1)
-    v.tensor_scalar(fb[:, 4:5], fb[:, 0:1], -1.0, fb[:, 1:2], A.mult, A.subtract).then_inc(S["fm"], 1)
+    s.activation(fb[:, 8:16], nbs, F.Exp, bias=fb[:, 0:1], scale=-1.0).then_inc(S["f2"], 1)
     v.wait_ge(S["f2"], 1)
-    v.tensor_tensor(fb[:, 16:24], fb[:, 8:16], T.st[:, 1:24:3], A.mult).then_inc(S["f4"], 1)
+    v.tensor_tensor(fb[:, 16:24], fb[:, 8:16], ss, A.mult).then_inc(S["f4"], 1)
     v.wait_ge(S["f4"], 1)
     v.tensor_reduce(fb[:, 2:3], fb[:, 16:24], X, A.add).then_inc(S["f5"], 1)
     v.wait_ge(S["f5"], 1)
     v.tensor_scalar(T.d0[:], T.e0[:], fb[:, 2:3], None, A.mult).then_inc(S["f6"], 1)
     v.wait_ge(S["f6"], 1)
     v.tensor_tensor_scan(T.sc[:], T.d0[:], T.d1[:], 0.0, A.mult, A.add).then_inc(S["f7"], 1)
+    v.wait_ge(S["ptt"], n_par)
+    v.tensor_reduce(fb[:, 1:2], T.st[:, 16:24], X, A.add).then_inc(S["f3"], 1)
+    v.tensor_scalar(fb[:, 5:6], fb[:, 0:1], -1.0, None, A.mult).then_inc(S["fm"], 1)
+    v.wait_ge(S["f3"], 1)
+    v.tensor_scalar(fb[:, 4:5], fb[:, 0:1], -1.0, fb[:, 1:2], A.mult, A.subtract).then_inc(S["fm"], 1)
     v.wait_ge(S["f7"], 1)
     v.tensor_reduce(fb[:, 3:4], T.sc[:, DEG:K * B:B], X, A.min).then_inc(S["f8"], 1)
     v.wait_ge(S["f8"], 1)

@@ -21,13 +21,14 @@ SCRATCH = {
     "ps": ("psum", [128, 4096], "float32"),
     "col": ("sbuf", [128, NC], "bfloat16"),
     "mk": ("sbuf", [128, 8 * NC], "bfloat16"),
-    "ex": ("sbuf", [128, 4 * NC], "float32"),
-    "pr": ("sbuf", [128, 4 * NC], "float32"),
+    "ex": ("sbuf", [128, 8 * NC], "float32"),
+    "pr": ("sbuf", [128, 8 * NC], "float32"),
     "vo": ("sbuf", [128, 4], "float32"),
     "vp": ("sbuf", [128, 4], "float32"),
     "mxb": ("sbuf", [128, 8], "float32"),
     "st": ("sbuf", [128, 24], "float32"),
     "sp": ("sbuf", [128, 12], "float32"),
+    "er": ("sbuf", [128, K * B], "float32"),
     "e0": ("sbuf", [128, K * B], "float32"),
     "d1": ("sbuf", [128, K * B], "float32"),
     "d0": ("sbuf", [128, K * B], "float32"),
@@ -35,10 +36,10 @@ SCRATCH = {
     "f": ("sbuf", [128, 32], "float32"),
     "yt": ("sbuf", [128, 4], "float32"),
 }
-TILES = [("o", 0), ("p", 0), ("p", 1), ("o", 1), ("p", 2), ("p", 3), ("o", 2), ("o", 3)]
-SEMAPHORES = (["lw", "lx", "lt", "qw", "qx", "io", "kc", "vo", "vp", "mko", "mkp", "loc", "rin", "rx",
+TILES = [("o", 0), ("o", 1), ("p", 0), ("p", 1), ("p", 2), ("p", 3), ("o", 2), ("o", 3)]
+SEMAPHORES = (["lw", "lx", "lt", "qw", "qx", "io", "k1", "k2", "k3", "kc", "vo", "vp", "mko", "mkp", "loc", "rin", "rx", "rt",
                "c1", "s1", "c2", "s2", "c3", "s3", "pxc", "pxs", "ptg", "pst", "ptt",
-               "f1", "f2", "f3", "f4", "f5", "f6", "f7", "f8", "f9", "fm", "stored"]
+               "f1", "f2", "f3", "f4", "f5", "f6", "f7", "f8", "f9", "fm", "fz", "stored"]
               + [n + str(i) for i in range(8) for n in ("mm", "mx", "nb", "ex", "pr", "cp")])
 
 
@@ -72,6 +73,10 @@ def hand(c, R, topo):
     return split(topo.mask(c, R["relay"][0][0]), 2)
 
 
+def rest(c, R, topo):
+    return split(topo.mask(c, R["relay"][0][0]) & ~topo.mask(c, R["sib"]), 2)
+
+
 def piece(T, kind, slot):
     if kind == "c":
         return T.wc[:, slot * NC:(slot + 1) * NC].bitcast(dt.uint8)
@@ -84,22 +89,24 @@ def relay_program(g, core, T, topo):
             continue
         R = roles(c, T, topo)
         for i, (h, dst, slot, kind) in enumerate(R["relay"]):
-            if h == core:
-                n = 0
-                if i < 2:
-                    p = R["partner"]
-                    m = topo.mask(core, p)
-                    rid, pid = topo.addr(p, core)
-                    g.wait_ge(T.sem["rx"], cnt(hand(c, R, topo)[i]))
-                    o = i * NX // 2
-                    g.remote_dma(T.xc[:, NX + o:NX + o + NX // 2].bitcast(dt.uint8), T.xc[:, o:o + NX // 2].bitcast(dt.uint8),
-                                 T.sem["pxc"], T.sem["loc"], pid, rid, m)
-                    n += cnt(m)
-                m = topo.mask(core, dst)
-                rid, pid = topo.addr(dst, core)
-                g.wait_ge(T.sem["rin"], cnt(hand(c, R, topo)[i % 2]))
-                g.remote_dma(piece(T, kind, slot), piece(T, kind, 0), T.sem[kind + str(slot)], T.sem["loc"], pid, rid, m)
-                g.wait_ge(T.sem["loc"], cnt(m) + n)
+            if h != core:
+                continue
+            p = R["partner"]
+            mp, md = topo.mask(core, p), topo.mask(core, dst)
+            rid, pid = topo.addr(p, core)
+            j = i % 2
+            if kind == "c":
+                g.wait_ge(T.sem["rt"], cnt(hand(c, R, topo)[j]))
+                g.remote_dma(T.tgp[:, j:j + 1], T.tgo[:, j:j + 1], T.sem["ptg"], T.sem["loc"], pid, rid, mp)
+            else:
+                g.wait_ge(T.sem["rx"], cnt(hand(c, R, topo)[j]))
+                o = j * NX // 2
+                g.remote_dma(T.xc[:, NX + o:NX + o + NX // 2].bitcast(dt.uint8), T.xc[:, o:o + NX // 2].bitcast(dt.uint8),
+                             T.sem["pxc"], T.sem["loc"], pid, rid, mp)
+            rid, pid = topo.addr(dst, core)
+            g.wait_ge(T.sem["rin"], cnt((hand if kind == "c" else rest)(c, R, topo)[j]))
+            g.remote_dma(piece(T, kind, slot), piece(T, kind, 0), T.sem[kind + str(slot)], T.sem["loc"], pid, rid, md)
+            g.wait_ge(T.sem["loc"], cnt(md) + cnt(mp))
 
 
 def rank_program(g, core, T, topo):
@@ -117,16 +124,16 @@ def rank_program(g, core, T, topo):
     rl = [r[0] for r in R["relay"]]
     n_par, n_sib = cnt(topo.mask(core, partner)), cnt(topo.mask(core, sib))
 
+    g.scalar.dma_start(T.tgo[:, 0:2], T.tg[:]).then_inc(S["lt"], 16)
     g.scalar.dma_start(T.xin[:], T.x[:]).then_inc(S["lx"], 16)
     g.sync.dma_start(T.win[:], T.w[:]).then_inc(S["lw"], 16)
-    g.sync.dma_start(T.tgo[:, 0:2], T.tg[:]).then_inc(S["lt"], 16)
 
     g.iota(T.col[:], [[1, NC]], 0, 0, allow_small_or_imprecise_dtypes=True).then_inc(S["io"], 1)
     local = [0]
 
-    def fused(sem, parts):
+    def fused(parts):
         tr = []
-        for (h, out, in_), m in zip(parts, hand(core, R, topo)):
+        for h, sem, out, in_, m in parts:
             rid, pid = topo.addr(h, core)
             tr.append(RemoteDMATransfer(dst_ids=[DstId(rid=rid, pnc=pid)], dma_engine_mask=m, remote_sem=S[sem], src=in_, dst=out))
             local[0] += cnt(m)
@@ -138,17 +145,18 @@ def rank_program(g, core, T, topo):
         g.remote_dma(out, in_, S[sem], S["loc"], pid, rid, m)
         local[0] += cnt(m)
 
-    g.wait_ge(S["qx"], 1)
-    fused("rx", [(rl[i], T.xc[:, i * NX // 2:(i + 1) * NX // 2].bitcast(dt.uint8),
-                  T.xc[:, i * NX // 2:(i + 1) * NX // 2].bitcast(dt.uint8)) for i in range(2)])
-    g.wait_ge(S["qw"], 1)
-    fused("rin", [(h, piece(T, "c", 0), piece(T, "c", 0)) for h in rl[0:2]])
-    fused("rin", [(h, piece(T, "s", 0), piece(T, "s", 0)) for h in rl[2:4]])
-    send(T.xs[:, NX:2 * NX], T.xs[:, 0:NX], "pxs", partner)
+    two, four = hand(core, R, topo), rest(core, R, topo)
+    half = [T.xc[:, i * NX // 2:(i + 1) * NX // 2].bitcast(dt.uint8) for i in range(2)]
     g.wait_ge(S["lt"], 16)
-    send(T.tgp[:, 0:2], T.tgo[:, 0:2], "ptg", partner)
+    fused([(rl[i], "rt", T.tgo[:, i:i + 1], T.tgo[:, i:i + 1], two[i]) for i in range(2)])
+    g.wait_ge(S["qw"], 1)
+    fused([(rl[i], "rin", piece(T, "c", 0), piece(T, "c", 0), two[i]) for i in range(2)])
+    g.wait_ge(S["qx"], 1)
+    fused([(rl[2 + i], "rx", half[i], half[i], two[i]) for i in range(2)])
+    fused([(rl[2 + i], "rin", piece(T, "s", 0), piece(T, "s", 0), four[i]) for i in range(2)]
+          + [(sib, "s1", piece(T, "s", 1), piece(T, "s", 0), topo.mask(core, sib))])
     send(piece(T, "c", 1), piece(T, "c", 0), "c1", sib)
-    send(piece(T, "s", 1), piece(T, "s", 0), "s1", sib)
+    send(T.xs[:, NX:2 * NX], T.xs[:, 0:NX], "pxs", partner)
     late = [i for i in range(8) if TILES[i][0] == "p"]
     for i in late:
         g.wait_ge(S["ex%d" % i], 1)
@@ -164,7 +172,7 @@ def rank_program(g, core, T, topo):
     seen = set()
     for i, (who, slot) in enumerate(TILES):
         if who == "p" and "p" not in seen:
-            g.tensor.wait_ge(S["pxc"], sum(cnt(topo.mask(h, partner)) for h in rl[0:2]))
+            g.tensor.wait_ge(S["pxc"], sum(cnt(topo.mask(h, partner)) for h in rl[2:4]))
             g.tensor.wait_ge(S["pxs"], n_par)
             seen.add("p")
         if slot and slot not in seen:
@@ -185,13 +193,30 @@ def rank_program(g, core, T, topo):
         return T.ps[:, 512 * i:512 * i + NC]
 
     def reg(buf, i):
-        return buf[:, (i % 4) * NC:(i % 4 + 1) * NC]
+        return buf[:, i * NC:(i + 1) * NC]
 
     def mask(who, slot):
         o = slot * NC + (0 if who == "o" else 4 * NC)
         return T.mk[:, o:o + NC]
 
     v = g.vector
+    s = g.scalar
+    coef = [0.0] * B
+    for n in range(1, B):
+        for j in range(n + 1):
+            coef[j] += (-1.0) ** (n + 1) / n * math.comb(n, j) * (-1.0) ** (n - j)
+    v.memset(T.er[:], 1.0).then_inc(S["k1"], 1)
+    for j in range(DEG):
+        v.memset(T.d1[:, j:K * B:B], coef[DEG - j]).then_inc(S["kc"], 1)
+    v.wait_ge(S["k1"], 1)
+    v.memset(T.er[:, B:K * B:B], math.exp(-STEP)).then_inc(S["k2"], 1)
+    v.wait_ge(S["k2"], 1)
+    v.tensor_tensor_scan(T.e0[:], T.er[:], T.er[:], 1.0, A.mult, A.min).then_inc(S["k3"], 1)
+    v.wait_ge(S["io"], 1)
+    v.tensor_scalar(T.d1[:, DEG:K * B:B], T.col[:, 0:K], STEP, coef[0], A.mult, A.add).then_inc(S["kc"], 1)
+    v.wait_ge(S["k3"], 1)
+    v.memset(T.e0[:, 0:K * B:B], 0.0).then_inc(S["kc"], 1)
+    nk = DEG + 2
     v.wait_ge(S["lx"], 16)
     v.quantize_mx(T.xc[:, 0:NX], T.xs[:, 0:NX], T.xin[:]).then_inc(S["qx"], 1)
     v.wait_ge(S["lw"], 16)
@@ -203,53 +228,43 @@ def rank_program(g, core, T, topo):
         for slot in range(4):
             v.tensor_scalar(mask(who, slot), T.col[:], float(NC * slot_rank[slot]), vbuf[:, 0:1], A.add, A.is_equal).then_inc(S[msem], 1)
 
-    coef = [0.0] * B
-    for n in range(1, B):
-        for j in range(n + 1):
-            coef[j] += (-1.0) ** (n + 1) / n * math.comb(n, j) * (-1.0) ** (n - j)
-    v.memset(T.e0[:, 0:K * B:B], 0.0).then_inc(S["kc"], 1)
-    for j in range(DEG):
-        v.memset(T.d1[:, j:K * B:B], coef[DEG - j]).then_inc(S["kc"], 1)
-    for k in range(K):
-        v.memset(T.e0[:, k * B + 1:(k + 1) * B], math.exp(-STEP * k)).then_inc(S["kc"], 1)
-        v.memset(T.d1[:, k * B + DEG:(k + 1) * B], coef[0] + STEP * k).then_inc(S["kc"], 1)
-    nk = 1 + DEG + 2 * K
-    v.wait_ge(S["io"], 1)
+    def peak(i):
+        v.wait_ge(S["mm%d" % i], 1)
+        v.tensor_reduce(T.mxb[:, i:i + 1], bank(i), X, A.max).then_inc(S["mx%d" % i], 1)
+        v.wait_ge(S["mx%d" % i], 1)
+        v.tensor_scalar(stat(*TILES[i], 0), T.mxb[:, i:i + 1], -SCALE, None, A.mult).then_inc(S["nb%d" % i], 1)
+
+    def pick(i):
+        v.wait_ge(S["ex%d" % i], 1)
+        v.tensor_tensor(reg(T.pr, i), bank(i), mask(*TILES[i]), A.mult).then_inc(S["pr%d" % i], 1)
+
+    def expsum(i):
+        s.wait_ge(S["nb%d" % i], 1)
+        s.activation(reg(T.ex, i), bank(i), F.Exp, bias=stat(*TILES[i], 0), scale=SCALE,
+                     accum_out=stat(*TILES[i], 1)).then_inc(S["ex%d" % i], 1)
+
+    def target(i):
+        s.wait_ge(S["pr%d" % i], 1)
+        s.activation(reg(T.pr, i), reg(T.pr, i), F.Copy, scale=SCALE, accum_out=stat(*TILES[i], 2)).then_inc(S["cp%d" % i], 1)
+
     v.wait_ge(S["lt"], 16)
     masks("o", T.tgo, T.vo, "vo", "mko")
-    v.wait_ge(S["ptg"], n_par)
+    peak(0)
+    v.wait_ge(S["ptg"], sum(cnt(topo.mask(h, partner)) for h in rl[0:2]))
     masks("p", T.tgp, T.vp, "vp", "mkp")
     v.wait_ge(S["mko"], 4)
     v.wait_ge(S["mkp"], 4)
-    for first in range(0, 8, 2):
-        for i in (first, first + 1):
-            who, slot = TILES[i]
-            v.wait_ge(S["mm%d" % i], 1)
-            v.tensor_reduce(T.mxb[:, i:i + 1], bank(i), X, A.max).then_inc(S["mx%d" % i], 1)
-            v.wait_ge(S["mx%d" % i], 1)
-            v.tensor_scalar(stat(who, slot, 0), T.mxb[:, i:i + 1], -SCALE, None, A.mult).then_inc(S["nb%d" % i], 1)
-        for i in (first, first + 1):
-            who, slot = TILES[i]
-            v.wait_ge(S["ex%d" % i], 1)
-            if i >= 4:
-                v.wait_ge(S["cp%d" % (i - 4)], 1)
-            v.tensor_tensor(reg(T.pr, i), bank(i), mask(who, slot), A.mult).then_inc(S["pr%d" % i], 1)
+    for job, i in ((pick, 0), (peak, 1), (peak, 2), (pick, 1), (pick, 2), (peak, 3), (pick, 3),
+                   (peak, 4), (peak, 5), (peak, 6), (peak, 7), (pick, 4), (pick, 5), (pick, 6), (pick, 7)):
+        job(i)
+    for job, i in ((expsum, 0), (target, 0), (expsum, 1), (expsum, 2), (target, 1), (target, 2), (expsum, 3), (target, 3),
+                   (expsum, 4), (expsum, 5), (expsum, 6), (expsum, 7), (target, 4), (target, 5), (target, 6)):
+        job(i)
 
-    s = g.scalar
-    for first in range(0, 8, 2):
-        for i in (first, first + 1):
-            who, slot = TILES[i]
-            s.wait_ge(S["nb%d" % i], 1)
-            s.activation(reg(T.ex, i), bank(i), F.Exp, bias=stat(who, slot, 0), scale=SCALE,
-                         accum_out=stat(who, slot, 1)).then_inc(S["ex%d" % i], 1)
-        for i in (first, first + 1):
-            who, slot = TILES[i]
-            s.wait_ge(S["pr%d" % i], 1)
-            s.activation(reg(T.pr, i), reg(T.pr, i), F.Copy, scale=SCALE, accum_out=stat(who, slot, 2)).then_inc(S["cp%d" % i], 1)
-
-    for i, (who, slot) in enumerate(TILES):
-        if who == "o":
-            v.wait_ge(S["cp%d" % i], 1)
+    own = [i for i in range(8) if TILES[i][0] == "o"]
+    for i in own:
+        v.wait_ge(S["nb%d" % i], 1)
+        v.wait_ge(S["ex%d" % i], 1)
     v.wait_ge(S["kc"], nk)
     v.wait_ge(S["pst"], n_par)
     fb = T.f
@@ -257,6 +272,8 @@ def rank_program(g, core, T, topo):
     v.tensor_reduce(fb[:, 0:1], nbs, X, A.min).then_inc(S["f1"], 1)
     s.wait_ge(S["f1"], 1)
     s.activation(fb[:, 8:16], nbs, F.Exp, bias=fb[:, 0:1], scale=-1.0).then_inc(S["f2"], 1)
+    v.wait_ge(S["f1"], 1)
+    v.tensor_scalar(fb[:, 5:6], fb[:, 0:1], -1.0, None, A.mult).then_inc(S["fz"], 1)
     v.wait_ge(S["f2"], 1)
     v.tensor_tensor(fb[:, 16:24], fb[:, 8:16], ss, A.mult).then_inc(S["f4"], 1)
     v.wait_ge(S["f4"], 1)
@@ -265,15 +282,19 @@ def rank_program(g, core, T, topo):
     v.tensor_scalar(T.d0[:], T.e0[:], fb[:, 2:3], None, A.mult).then_inc(S["f6"], 1)
     v.wait_ge(S["f6"], 1)
     v.tensor_tensor_scan(T.sc[:], T.d0[:], T.d1[:], 0.0, A.mult, A.add).then_inc(S["f7"], 1)
-    v.wait_ge(S["ptt"], n_par)
-    v.tensor_reduce(fb[:, 1:2], T.st[:, 16:24], X, A.add).then_inc(S["f3"], 1)
-    v.tensor_scalar(fb[:, 5:6], fb[:, 0:1], -1.0, None, A.mult).then_inc(S["fm"], 1)
-    v.wait_ge(S["f3"], 1)
-    v.tensor_scalar(fb[:, 4:5], fb[:, 0:1], -1.0, fb[:, 1:2], A.mult, A.subtract).then_inc(S["fm"], 1)
+    target(7)
+    for i in own:
+        s.wait_ge(S["cp%d" % i], 1)
+    s.wait_ge(S["ptt"], n_par)
+    s.activation(fb[:, 24:32], T.st[:, 16:24], F.Copy, accum_out=fb[:, 1:2]).then_inc(S["f3"], 1)
+    s.wait_ge(S["f3"], 1)
+    s.wait_ge(S["fz"], 1)
+    s.activation(fb[:, 4:5], fb[:, 1:2], F.Identity, bias=fb[:, 5:6], scale=-1.0).then_inc(S["fm"], 1)
     v.wait_ge(S["f7"], 1)
     v.tensor_reduce(fb[:, 3:4], T.sc[:, DEG:K * B:B], X, A.min).then_inc(S["f8"], 1)
     v.wait_ge(S["f8"], 1)
-    v.wait_ge(S["fm"], 2)
+    v.wait_ge(S["fz"], 1)
+    v.wait_ge(S["fm"], 1)
     v.tensor_scalar(T.yt[:, 0:2], fb[:, 4:6], fb[:, 3:4], None, A.add).then_inc(S["f9"], 1)
     g.sync.wait_ge(S["f9"], 1)
     g.sync.dma_start(T.y[:], T.yt[:, 0:2]).then_inc(S["stored"], 16)

import math
import numpy as np
from concourse.bass import DstId, RemoteDMATransfer
from concourse.mybir import dt, AluOpType, AxisListType, ActivationFunctionType

NC = 256
NX = 128
SCALE = float(np.float32(0.03))
K, DEG, STEP = 16, 7, 0.5
B = DEG + 1

SCRATCH = {
    "win": ("sbuf", [128, 4 * NC], "bfloat16"),
    "xin": ("sbuf", [128, 4 * NX], "bfloat16"),
    "tgo": ("sbuf", [128, 8], "bfloat16"),
    "tgp": ("sbuf", [128, 8], "bfloat16"),
    "wc": ("sbuf", [128, 4 * NC], "float8_e4m3fn_x4"),
    "ws": ("sbuf", [128, 4 * NC], "uint8"),
    "xc": ("sbuf", [128, 2 * NX], "float8_e4m3fn_x4"),
    "xs": ("sbuf", [128, 2 * NX], "uint8"),
    "ps": ("psum", [128, 4096], "float32"),
    "col": ("sbuf", [128, NC], "bfloat16"),
    "mk": ("sbuf", [128, 8 * NC], "bfloat16"),
    "ex": ("sbuf", [128, 8 * NC], "float32"),
    "pr": ("sbuf", [128, 8 * NC], "float32"),
    "vo": ("sbuf", [128, 4], "float32"),
    "vp": ("sbuf", [128, 4], "float32"),
    "mxb": ("sbuf", [128, 8], "float32"),
    "st": ("sbuf", [128, 24], "float32"),
    "sp": ("sbuf", [128, 12], "float32"),
    "er": ("sbuf", [128, K * B], "float32"),
    "e0": ("sbuf", [128, K * B], "float32"),
    "d1": ("sbuf", [128, K * B], "float32"),
    "d0": ("sbuf", [128, K * B], "float32"),
    "sc": ("sbuf", [128, K * B], "float32"),
    "f": ("sbuf", [128, 32], "float32"),
    "yt": ("sbuf", [128, 4], "float32"),
}
TILES = [("o", 0), ("o", 1), ("p", 0), ("p", 1), ("p", 2), ("p", 3), ("o", 2), ("o", 3)]
SEMAPHORES = (["lw", "lx", "lt", "qw", "qx", "io", "k1", "k2", "k3", "kc", "vo", "vp", "mko", "mkp", "loc", "rin", "rx", "rt",
               "c1", "s1", "c2", "s2", "c3", "s3", "pxc", "pxs", "ptg", "pst", "ptt",
               "f1", "f2", "f3", "f4", "f5", "f6", "f7", "f8", "f9", "fm", "fz", "stored"]
              + [n + str(i) for i in range(8) for n in ("mm", "mx", "nb", "ex", "pr", "cp")])


def roles(c, T, topo):
    rk = topo.rack(topo.host(c))
    near = [q for q in T.cores if q != c and topo.rack(topo.host(q)) == rk]
    sib = [q for q in near if topo.same_plane(c, q)][0]
    partner = [q for q in T.cores if topo.rack(topo.host(q)) != rk and topo.chip(q) == topo.chip(c) and topo.may_write(c, q)][0]
    cross = [q for q in near if not topo.same_plane(c, q)]
    same = [q for q in cross if topo.host(q) == topo.host(c)][0]
    other = [q for q in cross if topo.host(q) != topo.host(c)][0]
    base = [h for h in range(512) if topo.host(h) == topo.host(c) and topo.chip(h) == topo.chip(c) and T.rank_of(h) is None
            and topo.may_write(h, same) and topo.may_write(h, other)]
    mine = [h for h in base if topo.die(h) == topo.die(c)]
    far = [h for h in base if topo.die(h) != topo.die(c)]
    return {"sib": sib, "partner": partner, "same": same, "other": other,
            "relay": [(mine[0], same, 2, "c"), (far[0], other, 3, "c"), (mine[1], same, 2, "s"), (far[1], other, 3, "s")]}


def split(mask, n):
    bits = [b for b in range(16) if mask >> b & 1]
    k = len(bits) // n
    return [sum(1 << b for b in bits[i * k:(i + 1) * k]) for i in range(n)]


def cnt(mask):
    return bin(mask).count("1")


def hand(c, R, topo):
    return split(topo.mask(c, R["relay"][0][0]), 2)


def rest(c, R, topo):
    return split(topo.mask(c, R["relay"][0][0]) & ~topo.mask(c, R["sib"]), 2)


def piece(T, kind, slot):
    if kind == "c":
        return T.wc[:, slot * NC:(slot + 1) * NC].bitcast(dt.uint8)
    return T.ws[:, slot * NC:(slot + 1) * NC]


def relay_program(g, core, T, topo):
    for c in T.cores:
        if (topo.host(c), topo.chip(c)) != (topo.host(core), topo.chip(core)):
            continue
        R = roles(c, T, topo)
        for i, (h, dst, slot, kind) in enumerate(R["relay"]):
            if h != core:
                continue
            p = R["partner"]
            mp, md = topo.mask(core, p), topo.mask(core, dst)
            rid, pid = topo.addr(p, core)
            j = i % 2
            if kind == "c":
                g.wait_ge(T.sem["rt"], cnt(hand(c, R, topo)[j]))
                g.remote_dma(T.tgp[:, j:j + 1], T.tgo[:, j:j + 1], T.sem["ptg"], T.sem["loc"], pid, rid, mp)
            else:
                g.wait_ge(T.sem["rx"], cnt(hand(c, R, topo)[j]))
                o = j * NX // 2
                g.remote_dma(T.xc[:, NX + o:NX + o + NX // 2].bitcast(dt.uint8), T.xc[:, o:o + NX // 2].bitcast(dt.uint8),
                             T.sem["pxc"], T.sem["loc"], pid, rid, mp)
            rid, pid = topo.addr(dst, core)
            g.wait_ge(T.sem["rin"], cnt((hand if kind == "c" else rest)(c, R, topo)[j]))
            g.remote_dma(piece(T, kind, slot), piece(T, kind, 0), T.sem[kind + str(slot)], T.sem["loc"], pid, rid, md)
            g.wait_ge(T.sem["loc"], cnt(md) + cnt(mp))


def rank_program(g, core, T, topo):
    rank = T.rank_of(core)
    if rank is None:
        relay_program(g, core, T, topo)
        return
    R = roles(core, T, topo)
    S = T.sem
    A = AluOpType
    F = ActivationFunctionType
    X = AxisListType.X
    partner, sib = R["partner"], R["sib"]
    slot_rank = [T.rank_of(q) for q in (core, sib, R["same"], R["other"])]
    rl = [r[0] for r in R["relay"]]
    n_par, n_sib = cnt(topo.mask(core, partner)), cnt(topo.mask(core, sib))

    g.scalar.dma_start(T.tgo[:, 0:2], T.tg[:]).then_inc(S["lt"], 16)
    g.scalar.dma_start(T.xin[:], T.x[:]).then_inc(S["lx"], 16)
    g.sync.dma_start(T.win[:], T.w[:]).then_inc(S["lw"], 16)

    g.iota(T.col[:], [[1, NC]], 0, 0, allow_small_or_imprecise_dtypes=True).then_inc(S["io"], 1)
    local = [0]

    def fused(parts):
        tr = []
        for h, sem, out, in_, m in parts:
            rid, pid = topo.addr(h, core)
            tr.append(RemoteDMATransfer(dst_ids=[DstId(rid=rid, pnc=pid)], dma_engine_mask=m, remote_sem=S[sem], src=in_, dst=out))
            local[0] += cnt(m)
        g.remote_dma_fused(tr, local_sem=S["loc"])

    def send(out, in_, sem, dst):
        m = topo.mask(core, dst)
        rid, pid = topo.addr(dst, core)
        g.remote_dma(out, in_, S[sem], S["loc"], pid, rid, m)
        local[0] += cnt(m)

    two, four = hand(core, R, topo), rest(core, R, topo)
    half = [T.xc[:, i * NX // 2:(i + 1) * NX // 2].bitcast(dt.uint8) for i in range(2)]
    g.wait_ge(S["lt"], 16)
    fused([(rl[i], "rt", T.tgo[:, i:i + 1], T.tgo[:, i:i + 1], two[i]) for i in range(2)])
    g.wait_ge(S["qw"], 1)
    fused([(rl[i], "rin", piece(T, "c", 0), piece(T, "c", 0), two[i]) for i in range(2)])
    g.wait_ge(S["qx"], 1)
    fused([(rl[2 + i], "rx", half[i], half[i], two[i]) for i in range(2)])
    fused([(rl[2 + i], "rin", piece(T, "s", 0), piece(T, "s", 0), four[i]) for i in range(2)]
          + [(sib, "s1", piece(T, "s", 1), piece(T, "s", 0), topo.mask(core, sib))])
    send(piece(T, "c", 1), piece(T, "c", 0), "c1", sib)
    send(T.xs[:, NX:2 * NX], T.xs[:, 0:NX], "pxs", partner)
    late = [i for i in range(8) if TILES[i][0] == "p"]
    for i in late:
        g.wait_ge(S["ex%d" % i], 1)
    send(T.st[:, 8:16], T.sp[:, 0:8], "pst", partner)
    for i in late:
        g.wait_ge(S["cp%d" % i], 1)
    send(T.st[:, 20:24], T.sp[:, 8:12], "ptt", partner)
    g.wait_ge(S["loc"], local[0])

    g.tensor.wait_ge(S["qw"], 1)
    g.tensor.wait_ge(S["qx"], 1)
    n_in = {2: cnt(topo.mask(rl[0], R["same"])), 3: cnt(topo.mask(rl[1], R["other"])), 1: n_sib}
    seen = set()
    for i, (who, slot) in enumerate(TILES):
        if who == "p" and "p" not in seen:
            g.tensor.wait_ge(S["pxc"], sum(cnt(topo.mask(h, partner)) for h in rl[2:4]))
            g.tensor.wait_ge(S["pxs"], n_par)
            seen.add("p")
        if slot and slot not in seen:
            g.tensor.wait_ge(S["c%d" % slot], n_in[slot])
            g.tensor.wait_ge(S["s%d" % slot], n_in[slot])
            seen.add(slot)
        a, b = (0, NX) if who == "o" else (NX, 2 * NX)
        c, d = slot * NC, (slot + 1) * NC
        g.tensor.matmul_mx(T.ps[:, 512 * i:512 * i + NC], T.xc[:, a:b], T.xs[:, a:b], T.wc[:, c:d], T.ws[:, c:d],
                           True, True).then_inc(S["mm%d" % i], 1)

    def stat(who, slot, k):
        if k == 2:
            return T.st[:, 16 + slot:17 + slot] if who == "o" else T.sp[:, 8 + slot:9 + slot]
        return (T.st if who == "o" else T.sp)[:, 2 * slot + k:2 * slot + k + 1]

    def bank(i):
        return T.ps[:, 512 * i:512 * i + NC]

    def reg(buf, i):
        return buf[:, i * NC:(i + 1) * NC]

    def mask(who, slot):
        o = slot * NC + (0 if who == "o" else 4 * NC)
        return T.mk[:, o:o + NC]

    v = g.vector
    s = g.scalar
    coef = [0.0] * B
    for n in range(1, B):
        for j in range(n + 1):
            coef[j] += (-1.0) ** (n + 1) / n * math.comb(n, j) * (-1.0) ** (n - j)
    v.memset(T.er[:], 1.0).then_inc(S["k1"], 1)
    for j in range(DEG):
        v.memset(T.d1[:, j:K * B:B], coef[DEG - j]).then_inc(S["kc"], 1)
    v.wait_ge(S["k1"], 1)
    v.memset(T.er[:, B:K * B:B], math.exp(-STEP)).then_inc(S["k2"], 1)
    v.wait_ge(S["k2"], 1)
    v.tensor_tensor_scan(T.e0[:], T.er[:], T.er[:], 1.0, A.mult, A.min).then_inc(S["k3"], 1)
    v.wait_ge(S["io"], 1)
    v.tensor_scalar(T.d1[:, DEG:K * B:B], T.col[:, 0:K], STEP, coef[0], A.mult, A.add).then_inc(S["kc"], 1)
    v.wait_ge(S["k3"], 1)
    v.memset(T.e0[:, 0:K * B:B], 0.0).then_inc(S["kc"], 1)
    nk = DEG + 2
    v.wait_ge(S["lx"], 16)
    v.quantize_mx(T.xc[:, 0:NX], T.xs[:, 0:NX], T.xin[:]).then_inc(S["qx"], 1)
    v.wait_ge(S["lw"], 16)
    v.quantize_mx(T.wc[:, 0:NC], T.ws[:, 0:NC], T.win[:]).then_inc(S["qw"], 1)

    def masks(who, tgbuf, vbuf, vsem, msem):
        v.tensor_scalar(vbuf[:, 0:1], tgbuf[:, 0:1], float(NC), tgbuf[:, 1:2], A.mult, A.add).then_inc(S[vsem], 1)
        v.wait_ge(S[vsem], 1)
        for slot in range(4):
            v.tensor_scalar(mask(who, slot), T.col[:], float(NC * slot_rank[slot]), vbuf[:, 0:1], A.add, A.is_equal).then_inc(S[msem], 1)

    def peak(i):
        v.wait_ge(S["mm%d" % i], 1)
        v.tensor_reduce(T.mxb[:, i:i + 1], bank(i), X, A.max).then_inc(S["mx%d" % i], 1)
        v.wait_ge(S["mx%d" % i], 1)
        v.tensor_scalar(stat(*TILES[i], 0), T.mxb[:, i:i + 1], -SCALE, None, A.mult).then_inc(S["nb%d" % i], 1)

    def pick(i):
        v.wait_ge(S["ex%d" % i], 1)
        v.tensor_tensor(reg(T.pr, i), bank(i), mask(*TILES[i]), A.mult).then_inc(S["pr%d" % i], 1)

    def expsum(i):
        s.wait_ge(S["nb%d" % i], 1)
        s.activation(reg(T.ex, i), bank(i), F.Exp, bias=stat(*TILES[i], 0), scale=SCALE,
                     accum_out=stat(*TILES[i], 1)).then_inc(S["ex%d" % i], 1)

    def target(i):
        s.wait_ge(S["pr%d" % i], 1)
        s.activation(reg(T.pr, i), reg(T.pr, i), F.Copy, scale=SCALE, accum_out=stat(*TILES[i], 2)).then_inc(S["cp%d" % i], 1)

    v.wait_ge(S["lt"], 16)
    masks("o", T.tgo, T.vo, "vo", "mko")
    peak(0)
    v.wait_ge(S["ptg"], sum(cnt(topo.mask(h, partner)) for h in rl[0:2]))
    masks("p", T.tgp, T.vp, "vp", "mkp")
    v.wait_ge(S["mko"], 4)
    v.wait_ge(S["mkp"], 4)
    for job, i in ((pick, 0), (peak, 1), (peak, 2), (pick, 1), (pick, 2), (peak, 3), (pick, 3),
                   (peak, 4), (peak, 5), (peak, 6), (peak, 7), (pick, 4), (pick, 5), (pick, 6), (pick, 7)):
        job(i)
    for job, i in ((expsum, 0), (target, 0), (expsum, 1), (expsum, 2), (target, 1), (target, 2), (expsum, 3), (target, 3),
                   (expsum, 4), (expsum, 5), (expsum, 6), (expsum, 7), (target, 4), (target, 5), (target, 6)):
        job(i)

    own = [i for i in range(8) if TILES[i][0] == "o"]
    for i in own:
        v.wait_ge(S["nb%d" % i], 1)
        v.wait_ge(S["ex%d" % i], 1)
    v.wait_ge(S["kc"], nk)
    v.wait_ge(S["pst"], n_par)
    fb = T.f
    nbs, ss = T.st[:, 0:16:2], T.st[:, 1:16:2]
    v.tensor_reduce(fb[:, 0:1], nbs, X, A.min).then_inc(S["f1"], 1)
    s.wait_ge(S["f1"], 1)
    s.activation(fb[:, 8:16], nbs, F.Exp, bias=fb[:, 0:1], scale=-1.0).then_inc(S["f2"], 1)
    v.wait_ge(S["f1"], 1)
    v.tensor_scalar(fb[:, 5:6], fb[:, 0:1], -1.0, None, A.mult).then_inc(S["fz"], 1)
    v.wait_ge(S["f2"], 1)
    v.tensor_tensor(fb[:, 16:24], fb[:, 8:16], ss, A.mult).then_inc(S["f4"], 1)
    v.wait_ge(S["f4"], 1)
    v.tensor_reduce(fb[:, 2:3], fb[:, 16:24], X, A.add).then_inc(S["f5"], 1)
    v.wait_ge(S["f5"], 1)
    v.tensor_scalar(T.d0[:], T.e0[:], fb[:, 2:3], None, A.mult).then_inc(S["f6"], 1)
    v.wait_ge(S["f6"], 1)
    v.tensor_tensor_scan(T.sc[:], T.d0[:], T.d1[:], 0.0, A.mult, A.add).then_inc(S["f7"], 1)
    target(7)
    for i in own:
        s.wait_ge(S["cp%d" % i], 1)
    s.wait_ge(S["ptt"], n_par)
    s.activation(fb[:, 24:32], T.st[:, 16:24], F.Copy, accum_out=fb[:, 1:2]).then_inc(S["f3"], 1)
    s.wait_ge(S["f3"], 1)
    s.wait_ge(S["fz"], 1)
    s.activation(fb[:, 4:5], fb[:, 1:2], F.Identity, bias=fb[:, 5:6], scale=-1.0).then_inc(S["fm"], 1)
    v.wait_ge(S["f7"], 1)
    v.tensor_reduce(fb[:, 3:4], T.sc[:, DEG:K * B:B], X, A.min).then_inc(S["f8"], 1)
    v.wait_ge(S["f8"], 1)
    v.wait_ge(S["fz"], 1)
    v.wait_ge(S["fm"], 1)
    v.tensor_scalar(T.yt[:, 0:2], fb[:, 4:6], fb[:, 3:4], None, A.add).then_inc(S["f9"], 1)
    g.sync.wait_ge(S["f9"], 1)
    g.sync.dma_start(T.y[:], T.yt[:, 0:2]).then_inc(S["stored"], 16)
    g.sync.wait_ge(S["stored"], 16)
